import numpy as np
import ml_dtypes


def mxq(x, axis, fmt="e4m3"):
    dtype, down = {"e4m3": (ml_dtypes.float8_e4m3fn, 7), "e5m2": (ml_dtypes.float8_e5m2, 14)}[fmt]
    v = np.moveaxis(np.asarray(x, np.float32).astype(ml_dtypes.bfloat16).astype(np.float64), axis, -1)
    blocks = v.reshape(v.shape[:-1] + (-1, 32))
    amax = np.abs(blocks).max(-1, keepdims=True)
    byte = np.maximum(np.where(amax > 0, np.frexp(amax)[1] - 1 + 127, 0) - down, 1)
    scale = np.exp2(byte - 127.0)
    codes = (blocks / scale).astype(np.float32).astype(dtype).astype(np.float64)
    return np.moveaxis((codes * scale).reshape(v.shape), -1, axis)


WIDE = False


def mx_kscale(k):
    if not WIDE:
        return np.ones(k)
    levels = np.array([30, -30])
    if k % 512:
        return np.exp2(np.random.permutation(np.resize(levels, k // 32))).repeat(32)
    a = np.empty((k // 512, 16))
    for p in range(k // 512):
        a[p, :8] = np.random.permutation(np.resize(levels, 8))
        for g in range(8):
            far = levels[np.abs(levels - a[p, g]) >= 10]
            a[p, g + 8] = far[np.random.randint(len(far))]
    return np.exp2(a.ravel()).repeat(32)


def f64(x):
    return np.asarray(x).astype(np.float64)


def striped(idx):
    return np.tile(np.asarray(idx).reshape(-1, 16).T, (8, 1)).astype(np.uint16)


def unstriped(offs):
    return offs[:16].T.reshape(-1).astype(np.int64)


def bf(x):
    return np.asarray(x, np.float32).astype(ml_dtypes.bfloat16)


def planes(Y):
    r, m = Y.shape
    b = f64(bf(Y)).reshape(r // 32, 32, m)
    amax = np.abs(b).max(1)
    byte = np.clip(np.where(amax > 0, np.frexp(amax)[1] - 1 + 127 - 7, 1), 1, 254)
    codes = (b * np.exp2(127.0 - byte)[:, None, :]).reshape(r, m).astype(np.float32).astype(ml_dtypes.float8_e4m3fn).view(np.uint8)
    words = codes.reshape(r // 512, 128, 4, m).transpose(0, 1, 3, 2)
    return np.ascontiguousarray(words), np.ascontiguousarray(byte.astype(np.uint8).reshape(r // 512, 16, m))


K, N, T, S, J, B = 512, 512, 1024, 1024, 2048, 512


def setup_inputs():
    n = np.random.standard_normal
    idx = np.random.randint(0, T, J)
    idx2 = np.random.randint(0, S, J)
    fb = mx_kscale(B)
    return {
        "xf": (n((K, T))).astype(np.float32),
        "xo": (n((N, S))).astype(np.float32),
        "ra": (np.random.uniform(0.3, 1.0, (1, B)) * fb).astype(np.float32),
        "rb": (np.random.uniform(0.3, 1.0, (1, B)) / fb).astype(np.float32),
        "offs": striped(idx),
        "offs2": striped(idx2),
    }


def reference(xf, xo, ra, rb, offs, offs2):
    idx = unstriped(offs)
    idx2 = unstriped(offs2)
    sa = f64(xf)[:, idx].reshape(K, B, J // B).sum(axis=2) * f64(ra)
    sb = f64(xo)[:, idx2].reshape(N, B, J // B).sum(axis=2) * f64(rb)
    at = sa.T
    bt = sb.T
    atq = mxq(at, 0, "e4m3")
    btq = mxq(bt, 0, "e5m2")
    w = atq.T @ btq
    y = 0.03 * w
    words, scales = planes(y)
    return y, words, scales

@@ -1,0 +1,209 @@
+from contextlib import ExitStack
+
+import concourse.mybir as mybir
+from concourse.masks import make_identity
+
+K, N, T, J, B = 512, 512, 1024, 2048, 512
+FLOPS = 2 * K * N * B
+
+F32 = mybir.dt.float32
+BF16 = mybir.dt.bfloat16
+I32 = mybir.dt.int32
+U32 = mybir.dt.uint32
+U16 = mybir.dt.uint16
+U8 = mybir.dt.uint8
+E4M3 = mybir.dt.float8_e4m3fn_x4
+E5M2 = mybir.dt.float8_e5m2_x4
+COPY = mybir.ActivationFunctionType.Copy
+MULT = mybir.AluOpType.mult
+
+P = 128
+PACK = 4
+GROUP = J // B
+SLOTS = PACK * GROUP
+PLANES = 8
+TAIL = 16
+OUT_SCALE = 0.03
+LAST_PIECES = (56, 36, 24, 12)
+
+
+def tile_moe_expert_group_sums_wgrad_pl_kernel(tc, xf, xo, ra, rb, offs, offs2, out_0, out_1, out_2):
+    nc = tc.nc
+    with ExitStack() as ctx:
+        keep = ctx.enter_context(tc.tile_pool(name="keep", bufs=1))
+        psum = ctx.enter_context(tc.psum_pool(name="psum", bufs=1))
+
+        list_f = keep.tile([P, J // 16], U16, name="list_f")
+        list_o = keep.tile([P, J // 16], U16, name="list_o")
+        windows = [keep.tile([P, T + TAIL], F32, name="window%d" % q) for q in range(PLANES)]
+        weight_f = keep.tile([P, PACK], F32, name="weight_f")
+        weight_o = keep.tile([P, PACK], F32, name="weight_o")
+        ident = keep.tile([P, P], F32, name="ident")
+
+        xo_planes = xo.rearrange("(c p) s -> c p s", p=P)
+        xf_planes = xf.rearrange("(p t) s -> t p s", t=PACK)
+        sources = [xo_planes[c] for c in range(4)] + [xf_planes[t] for t in range(4)]
+        lists = [list_o] * 4 + [list_f] * 4
+        weights = [weight_o] * 4 + [weight_f] * 4
+
+        nc.sync.dma_start(list_o[:], offs2)
+        nc.sync.dma_start(out=windows[0][:, 0:T], in_=sources[0])
+        nc.sync.dma_start(out=windows[1][:, 0:T], in_=sources[1])
+        nc.sync.dma_start(out=weight_o[:], in_=rb.rearrange("o (p t) -> (o p) t", t=PACK))
+        nc.sync.dma_start(out=windows[2][:, 0:T], in_=sources[2])
+        nc.sync.dma_start(out=windows[3][:, 0:T], in_=sources[3])
+        nc.sync.dma_start(list_f[:], offs)
+        nc.sync.dma_start(out=weight_f[:], in_=ra.rearrange("o (p t) -> (o p) t", t=PACK))
+        for q in range(4, PLANES):
+            nc.sync.dma_start(out=windows[q][:, 0:T], in_=sources[q])
+        for q in range(PLANES):
+            nc.vector.memset(windows[q][:, T : T + TAIL], 0.0)
+        make_identity(nc, ident[:])
+
+        arena = keep.tile([P, (PLANES + 1) * J], F32, name="arena", align_bytes=64)
+        gathered = [arena[:, q * J : (q + 1) * J] for q in range(PLANES - 1)]
+        starts = [sum(LAST_PIECES[:u]) for u in range(len(LAST_PIECES))]
+        sorted_at = (PLANES - 1) * J + 16 * LAST_PIECES[0]
+        sorted_last = arena[:, sorted_at : sorted_at + J].rearrange("k (s p) -> k s p", p=P)
+        place = [(PLANES - 1) * J] + [PLANES * J + 16 * s for s in starts[1:]]
+        pieces = [arena[:, place[u] : place[u] + 16 * LAST_PIECES[u]] for u in range(len(LAST_PIECES))]
+
+        staged = [arena[:, (q + 3) * J - 128 : (q + 3) * J + 128].bitcast(BF16) for q in range(5)]
+        apart = place[3] - place[1]
+        staged5 = arena[:, place[1] - 64 : place[1] - 64 + apart + 128]
+        staged5_halves = [staged5[:, 0:128].bitcast(BF16), staged5[:, apart : apart + 128].bitcast(BF16)]
+        staged.append(None)
+        staged6 = keep.tile([P, P * PACK], BF16, name="staged6", align_bytes=64)
+        staged7 = keep.tile([P, P * PACK], BF16, name="staged7", align_bytes=64)
+        staged.extend([staged6[:], staged7[:]])
+
+        b_codes = keep.tile([P, N], U32, name="b_codes", align_bytes=64)
+        b_scales = keep.tile([P, N], U8, name="b_scales", align_bytes=64)
+        a_codes = [keep.tile([P, P], U32, name="a_codes%d" % t, align_bytes=64) for t in range(PACK)]
+        a_scales = [keep.tile([P, P], U8, name="a_scales%d" % t, align_bytes=64) for t in range(PACK)]
+
+        y = keep.tile([P, PACK, N], F32, name="y")
+        y_round = keep.tile([P, N, PACK], BF16, name="y_round", align_bytes=64)
+        y_codes = keep.tile([P, N], U32, name="y_codes", align_bytes=64)
+        y_scales = keep.tile([P, N], U8, name="y_scales", align_bytes=64)
+        out_rows = out_0.rearrange("(m t) n -> t m n", t=PACK)
+        out_words = out_1.rearrange("z l c r -> (z l) (c r)").bitcast(I32)
+        out_scales = out_2.rearrange("z q c -> (z q) c").bitcast(I32)
+
+        def gather(q, out, first, columns):
+            nc.vector.tensor_copy(out, windows[q][:].indirect(lists[q][:, first : first + columns]))
+
+        def add_transposes(bank, columns_of_slot, t):
+            for i in range(GROUP):
+                nc.tensor.matmul(bank, lhsT=columns_of_slot(GROUP * t + i), rhs=ident[:], is_transpose=True,
+                                 start=(i == 0), stop=(i == GROUP - 1))
+
+        def turn_by_groups(q):
+            slots = gathered[q].rearrange("k (p s) -> k s p", s=SLOTS)
+            for t in range(PACK):
+                bank = psum.tile([P, P], F32, name="group_bank", tag="group_bank", bufs=4)
+                add_transposes(bank[:], lambda s: slots[:, s, :], t)
+                if q < 5:
+                    words = staged[q].rearrange("p (k t) -> p t k", t=PACK)
+                    nc.scalar.activation(words[:, t, :], bank[:], COPY, scale=weights[q][:, t : t + 1])
+                else:
+                    for h in range(2):
+                        words = staged5_halves[h].rearrange("p (k t) -> p t k", t=PACK)
+                        nc.scalar.activation(words[:, t, :], bank[:, 64 * h : 64 * (h + 1)], COPY,
+                                             scale=weights[q][:, t : t + 1])
+
+        def turn_whole(slots):
+            bank = psum.tile([P, PACK, P], F32, name="plane_bank", tag="plane_bank", bufs=2)
+            for t in range(PACK):
+                add_transposes(bank[:, t, :], lambda s: slots[:, s, :], t)
+            return bank
+
+        def weigh_whole(q, bank):
+            nc.vector.tensor_tensor(
+                staged[q].rearrange("p (k t) -> p k t", t=PACK),
+                bank[:].rearrange("p t k -> p k t"),
+                weights[q][:].unsqueeze(1).to_broadcast([P, P, PACK]),
+                MULT,
+            )
+
+        def quantize(q):
+            if q < 4:
+                cols = slice(q * P, (q + 1) * P)
+                nc.vector.quantize_mx(out=b_codes[:, cols].bitcast(E5M2), scales=b_scales[:, cols], in_=staged[q])
+            elif q == 5:
+                for h in range(2):
+                    cols = slice(64 * h, 64 * (h + 1))
+                    nc.vector.quantize_mx(out=a_codes[1][:, cols].bitcast(E4M3), scales=a_scales[1][:, cols],
+                                          in_=staged5_halves[h])
+            else:
+                nc.vector.quantize_mx(out=a_codes[q - 4][:].bitcast(E4M3), scales=a_scales[q - 4][:], in_=staged[q])
+
+        def product(t):
+            acc = psum.tile([P, N], F32, name="acc", tag="acc", bufs=2)
+            nc.tensor.matmul_mx(out=acc[:], lhsT=a_codes[t][:].bitcast(E4M3), lhsT_scale=a_scales[t][:],
+                                rhs=b_codes[:].bitcast(E5M2), rhs_scale=b_scales[:], start=True, stop=True)
+            return acc
+
+        def scale_out(t, acc, cols):
+            nc.scalar.activation(y[:, t, cols], acc[:, cols], COPY, scale=OUT_SCALE)
+
+        def store_rows(t):
+            nc.sync.dma_start(out=out_rows[t], in_=y[:, t, :])
+
+        def round_pair(t, cols):
+            nc.vector.tensor_copy(y_round[:, cols, t : t + 2], y[:, t : t + 2, cols].rearrange("p t n -> p n t"))
+
+        whole = slice(0, N)
+        halves = (slice(0, N // 2), slice(N // 2, N))
+
+        for q in range(PLANES - 1):
+            gather(q, gathered[q][:, 0 : J // 2], 0, 64)
+            if q >= 2:
+                quantize(q - 2)
+            gather(q, gathered[q][:, J // 2 : J], 64, 64)
+            if q == 6:
+                scale_out(0, product(0), whole)
+                store_rows(0)
+            if q < 6:
+                turn_by_groups(q)
+        bank6 = turn_whole(gathered[6].rearrange("k (p s) -> k s p", s=SLOTS))
+
+        def gather_piece(u):
+            gather(7, pieces[u], starts[u], LAST_PIECES[u])
+
+        def sort_piece(u):
+            nc.scalar.copy(
+                sorted_last[:, :, starts[u] : starts[u] + LAST_PIECES[u]].rearrange("k (t i) (h l) -> k t h i l", i=4, l=4),
+                pieces[u].rearrange("k (h l t i) -> k t h i l", l=4, t=4, i=4),
+            )
+
+        gather_piece(0)
+        quantize(5)
+        sort_piece(0)
+        for u in range(1, len(LAST_PIECES)):
+            gather_piece(u)
+            sort_piece(u)
+        scale_out(1, product(1), whole)
+        store_rows(1)
+        weigh_whole(6, bank6)
+        quantize(6)
+        round_pair(0, whole)
+        bank7 = turn_whole(sorted_last)
+        scale_out(2, product(2), whole)
+        store_rows(2)
+        weigh_whole(7, bank7)
+        quantize(7)
+        acc3 = product(3)
+        for cols in halves:
+            scale_out(3, acc3, cols)
+        store_rows(3)
+        for cols in halves:
+            round_pair(2, cols)
+        for cols in halves:
+            nc.vector.quantize_mx(out=y_codes[:, cols].bitcast(E4M3), scales=y_scales[:, cols],
+                                  in_=y_round[:, cols, :].rearrange("p n t -> p (n t)"))
+            nc.sync.dma_start(out=out_words[:, cols], in_=y_codes[:, cols].bitcast(I32))
+        for quad in range(4):
+            queue = nc.scalar if quad < 2 else nc.sync
+            queue.dma_start(out=out_scales[4 * quad : 4 * quad + 4, :],
+                            in_=y_scales[32 * quad : 32 * quad + 4, :].bitcast(I32))

@@ -60,22 +60,22 @@ def tile_moe_expert_group_sums_wgrad_pl_kernel(tc, xf, xo, ra, rb, offs, offs2, 
             nc.vector.memset(windows[q][:, T : T + TAIL], 0.0)
         make_identity(nc, ident[:])
 
-        arena = keep.tile([P, (PLANES + 1) * J], F32, name="arena", align_bytes=64)
-        gathered = [arena[:, q * J : (q + 1) * J] for q in range(PLANES - 1)]
+        gathered = [keep.tile([P, J], F32, name="gathered%d" % q) for q in range(PLANES - 1)]
         starts = [sum(LAST_PIECES[:u]) for u in range(len(LAST_PIECES))]
-        sorted_at = (PLANES - 1) * J + 16 * LAST_PIECES[0]
-        sorted_last = arena[:, sorted_at : sorted_at + J].rearrange("k (s p) -> k s p", p=P)
-        place = [(PLANES - 1) * J] + [PLANES * J + 16 * s for s in starts[1:]]
-        pieces = [arena[:, place[u] : place[u] + 16 * LAST_PIECES[u]] for u in range(len(LAST_PIECES))]
+        last = keep.tile([P, J + 64], F32, name="last", align_bytes=64)
+        pieces = [last[:, 16 * starts[u] : 16 * (starts[u] + LAST_PIECES[u])] for u in range(len(LAST_PIECES))]
+        half = J // 2
+        arena = keep.tile([P, half + J], F32, name="arena")
+        sorted_of = [arena[:, half // 2 : half // 2 + half]] * 6 + [arena[:, 0:half], arena[:, half : half + J]]
+        sorted_of = [s.rearrange("k (s p) -> k s p", p=P) for s in sorted_of]
 
-        staged = [arena[:, (q + 3) * J - 128 : (q + 3) * J + 128].bitcast(BF16) for q in range(5)]
-        apart = place[3] - place[1]
-        staged5 = arena[:, place[1] - 64 : place[1] - 64 + apart + 128]
-        staged5_halves = [staged5[:, 0:128].bitcast(BF16), staged5[:, apart : apart + 128].bitcast(BF16)]
-        staged.append(None)
-        staged6 = keep.tile([P, P * PACK], BF16, name="staged6", align_bytes=64)
-        staged7 = keep.tile([P, P * PACK], BF16, name="staged7", align_bytes=64)
-        staged.extend([staged6[:], staged7[:]])
+        staged_o = keep.tile([P, N * PACK], BF16, name="staged_o", align_bytes=64)
+        staged = [staged_o[:, q * P * PACK : (q + 1) * P * PACK] for q in range(4)]
+        for q in range(4, PLANES):
+            if q == 6:
+                staged.append(last[:, J - 192 : J + 64].bitcast(BF16))
+            else:
+                staged.append(keep.tile([P, P * PACK], BF16, name="staged%d" % q, align_bytes=64)[:])
 
         b_codes = keep.tile([P, N], U32, name="b_codes", align_bytes=64)
         b_scales = keep.tile([P, N], U8, name="b_scales", align_bytes=64)
@@ -93,30 +93,32 @@ def tile_moe_expert_group_sums_wgrad_pl_kernel(tc, xf, xo, ra, rb, offs, offs2, 
         def gather(q, out, first, columns):
             nc.vector.tensor_copy(out, windows[q][:].indirect(lists[q][:, first : first + columns]))
 
-        def add_transposes(bank, columns_of_slot, t):
-            for i in range(GROUP):
-                nc.tensor.matmul(bank, lhsT=columns_of_slot(GROUP * t + i), rhs=ident[:], is_transpose=True,
-                                 start=(i == 0), stop=(i == GROUP - 1))
+        def bank_tile(index, shape):
+            return psum.tile(shape, F32, name="bank%d" % index, tag="bank%d" % index)
 
-        def turn_by_groups(q):
-            slots = gathered[q].rearrange("k (p s) -> k s p", s=SLOTS)
+        def sort_half(q, u):
+            nc.scalar.copy(
+                sorted_of[q][:, :, 64 * u : 64 * (u + 1)].rearrange("k (t i) (h l) -> k t h i l", i=4, l=4),
+                gathered[q][:, half * u : half * (u + 1)].rearrange(
+                    "k (h l v t i) -> k v t h i l", l=4, v=2, t=2, i=4)[:, 0],
+            )
+
+        def turn(q):
+            bank = bank_tile(q % 4, [P, PACK, P])
             for t in range(PACK):
-                bank = psum.tile([P, P], F32, name="group_bank", tag="group_bank", bufs=4)
-                add_transposes(bank[:], lambda s: slots[:, s, :], t)
-                if q < 5:
-                    words = staged[q].rearrange("p (k t) -> p t k", t=PACK)
-                    nc.scalar.activation(words[:, t, :], bank[:], COPY, scale=weights[q][:, t : t + 1])
+                if q == 7 or t < 2:
+                    slots = sorted_of[q]
                 else:
-                    for h in range(2):
-                        words = staged5_halves[h].rearrange("p (k t) -> p t k", t=PACK)
-                        nc.scalar.activation(words[:, t, :], bank[:, 64 * h : 64 * (h + 1)], COPY,
-                                             scale=weights[q][:, t : t + 1])
-
-        def turn_whole(slots):
-            bank = psum.tile([P, PACK, P], F32, name="plane_bank", tag="plane_bank", bufs=2)
-            for t in range(PACK):
-                add_transposes(bank[:, t, :], lambda s: slots[:, s, :], t)
+                    slots = gathered[q][:].rearrange("k (p s) -> k s p", s=SLOTS)
+                for i in range(GROUP):
+                    nc.tensor.matmul(bank[:, t, :], lhsT=slots[:, GROUP * t + i, :], rhs=ident[:], is_transpose=True,
+                                     start=(i == 0), stop=(i == GROUP - 1))
             return bank
+
+        def weigh_by_slots(q, bank):
+            words = staged[q].rearrange("p (k t) -> p t k", t=PACK)
+            for t in range(PACK):
+                nc.scalar.activation(words[:, t, :], bank[:, t, :], COPY, scale=weights[q][:, t : t + 1])
 
         def weigh_whole(q, bank):
             nc.vector.tensor_tensor(
@@ -127,19 +129,10 @@ def tile_moe_expert_group_sums_wgrad_pl_kernel(tc, xf, xo, ra, rb, offs, offs2, 
             )
 
         def quantize(q):
-            if q < 4:
-                cols = slice(q * P, (q + 1) * P)
-                nc.vector.quantize_mx(out=b_codes[:, cols].bitcast(E5M2), scales=b_scales[:, cols], in_=staged[q])
-            elif q == 5:
-                for h in range(2):
-                    cols = slice(64 * h, 64 * (h + 1))
-                    nc.vector.quantize_mx(out=a_codes[1][:, cols].bitcast(E4M3), scales=a_scales[1][:, cols],
-                                          in_=staged5_halves[h])
-            else:
-                nc.vector.quantize_mx(out=a_codes[q - 4][:].bitcast(E4M3), scales=a_scales[q - 4][:], in_=staged[q])
+            nc.vector.quantize_mx(out=a_codes[q - 4][:].bitcast(E4M3), scales=a_scales[q - 4][:], in_=staged[q])
 
-        def product(t):
-            acc = psum.tile([P, N], F32, name="acc", tag="acc", bufs=2)
+        def product(t, index):
+            acc = bank_tile(index, [P, N])
             nc.tensor.matmul_mx(out=acc[:], lhsT=a_codes[t][:].bitcast(E4M3), lhsT_scale=a_scales[t][:],
                                 rhs=b_codes[:].bitcast(E5M2), rhs_scale=b_scales[:], start=True, stop=True)
             return acc
@@ -156,44 +149,36 @@ def tile_moe_expert_group_sums_wgrad_pl_kernel(tc, xf, xo, ra, rb, offs, offs2, 
         whole = slice(0, N)
         halves = (slice(0, N // 2), slice(N // 2, N))
 
+        banks = {}
         for q in range(PLANES - 1):
-            gather(q, gathered[q][:, 0 : J // 2], 0, 64)
-            if q >= 2:
-                quantize(q - 2)
-            gather(q, gathered[q][:, J // 2 : J], 64, 64)
-            if q == 6:
-                scale_out(0, product(0), whole)
-                store_rows(0)
-            if q < 6:
-                turn_by_groups(q)
-        bank6 = turn_whole(gathered[6].rearrange("k (p s) -> k s p", s=SLOTS))
-
-        def gather_piece(u):
+            for u in range(2):
+                gather(q, gathered[q][:, half * u : half * (u + 1)], 64 * u, 64)
+                sort_half(q, u)
+            if 1 <= q <= 5:
+                weigh_by_slots(q - 1, banks[q - 1])
+            banks[q] = turn(q)
+        for u in range(len(LAST_PIECES)):
             gather(7, pieces[u], starts[u], LAST_PIECES[u])
-
-        def sort_piece(u):
             nc.scalar.copy(
-                sorted_last[:, :, starts[u] : starts[u] + LAST_PIECES[u]].rearrange("k (t i) (h l) -> k t h i l", i=4, l=4),
+                sorted_of[7][:, :, starts[u] : starts[u] + LAST_PIECES[u]].rearrange(
+                    "k (t i) (h l) -> k t h i l", i=4, l=4),
                 pieces[u].rearrange("k (h l t i) -> k t h i l", l=4, t=4, i=4),
             )
-
-        gather_piece(0)
-        quantize(5)
-        sort_piece(0)
-        for u in range(1, len(LAST_PIECES)):
-            gather_piece(u)
-            sort_piece(u)
-        scale_out(1, product(1), whole)
-        store_rows(1)
-        weigh_whole(6, bank6)
+        banks[7] = turn(7)
+        weigh_by_slots(5, banks[5])
+        nc.vector.quantize_mx(out=b_codes[:].bitcast(E5M2), scales=b_scales[:], in_=staged_o[:])
+        quantize(4)
+        weigh_whole(6, banks[6])
         quantize(6)
-        round_pair(0, whole)
-        bank7 = turn_whole(sorted_last)
-        scale_out(2, product(2), whole)
-        store_rows(2)
-        weigh_whole(7, bank7)
+        quantize(5)
+        weigh_whole(7, banks[7])
         quantize(7)
-        acc3 = product(3)
+        for t, index in ((0, 1), (1, 4), (2, 5)):
+            scale_out(t, product(t, index), whole)
+            store_rows(t)
+            if t == 1:
+                round_pair(0, whole)
+        acc3 = product(3, 6)
         for cols in halves:
             scale_out(3, acc3, cols)
         store_rows(3)

@@ -22,7 +22,6 @@ PACK = 4
 GROUP = J // B
 SLOTS = PACK * GROUP
 PLANES = 8
-TAIL = 16
 OUT_SCALE = 0.03
 LAST_PIECES = (56, 36, 24, 12)
 
@@ -35,7 +34,11 @@ def tile_moe_expert_group_sums_wgrad_pl_kernel(tc, xf, xo, ra, rb, offs, offs2, 
 
         list_f = keep.tile([P, J // 16], U16, name="list_f")
         list_o = keep.tile([P, J // 16], U16, name="list_o")
-        windows = [keep.tile([P, T + TAIL], F32, name="window%d" % q) for q in range(PLANES)]
+        table_o = keep.tile([P, 6 * T], F32, name="table_o")
+        table_f = keep.tile([P, 5 * T], F32, name="table_f")
+        tables = [table_o] * 4 + [table_f] * 4
+        origin = [3 * T, 2 * T, T, 0, 0, T, 2 * T, 3 * T]
+        windows = [tables[q][:, origin[q] : origin[q] + T] for q in range(PLANES)]
         weight_f = keep.tile([P, PACK], F32, name="weight_f")
         weight_o = keep.tile([P, PACK], F32, name="weight_o")
         ident = keep.tile([P, P], F32, name="ident")
@@ -47,33 +50,36 @@ def tile_moe_expert_group_sums_wgrad_pl_kernel(tc, xf, xo, ra, rb, offs, offs2, 
         weights = [weight_o] * 4 + [weight_f] * 4
 
         nc.sync.dma_start(list_o[:], offs2)
-        nc.sync.dma_start(out=windows[0][:, 0:T], in_=sources[0])
-        nc.sync.dma_start(out=windows[1][:, 0:T], in_=sources[1])
+        nc.sync.dma_start(out=windows[0], in_=sources[0])
+        nc.sync.dma_start(out=windows[1], in_=sources[1])
         nc.sync.dma_start(out=weight_o[:], in_=rb.rearrange("o (p t) -> (o p) t", t=PACK))
-        nc.sync.dma_start(out=windows[2][:, 0:T], in_=sources[2])
-        nc.sync.dma_start(out=windows[3][:, 0:T], in_=sources[3])
+        nc.sync.dma_start(out=windows[2], in_=sources[2])
+        nc.sync.dma_start(out=windows[3], in_=sources[3])
         nc.sync.dma_start(list_f[:], offs)
         nc.sync.dma_start(out=weight_f[:], in_=ra.rearrange("o (p t) -> (o p) t", t=PACK))
         for q in range(4, PLANES):
-            nc.sync.dma_start(out=windows[q][:, 0:T], in_=sources[q])
-        for q in range(PLANES):
-            nc.vector.memset(windows[q][:, T : T + TAIL], 0.0)
+            nc.sync.dma_start(out=windows[q], in_=sources[q])
+        nc.vector.memset(table_o[:, 4 * T : 6 * T], 0.0)
+        nc.vector.memset(table_f[:, 4 * T : 5 * T], 0.0)
         make_identity(nc, ident[:])
 
         gathered = [keep.tile([P, J], F32, name="gathered%d" % q) for q in range(PLANES - 1)]
         starts = [sum(LAST_PIECES[:u]) for u in range(len(LAST_PIECES))]
-        last = keep.tile([P, J + 64], F32, name="last", align_bytes=64)
+        last = keep.tile([P, J + 192], F32, name="last", align_bytes=64)
         pieces = [last[:, 16 * starts[u] : 16 * (starts[u] + LAST_PIECES[u])] for u in range(len(LAST_PIECES))]
-        half = J // 2
-        arena = keep.tile([P, half + J], F32, name="arena")
-        sorted_of = [arena[:, half // 2 : half // 2 + half]] * 6 + [arena[:, 0:half], arena[:, half : half + J]]
+        quarter = J // 4
+        arena = keep.tile([P, quarter + J], F32, name="arena")
+        sorted_of = [arena[:, quarter // 2 : quarter // 2 + quarter]] * 6
+        sorted_of = sorted_of + [arena[:, 0:quarter], arena[:, quarter : quarter + J]]
         sorted_of = [s.rearrange("k (s p) -> k s p", p=P) for s in sorted_of]
 
         staged_o = keep.tile([P, N * PACK], BF16, name="staged_o", align_bytes=64)
         staged = [staged_o[:, q * P * PACK : (q + 1) * P * PACK] for q in range(4)]
         for q in range(4, PLANES):
-            if q == 6:
-                staged.append(last[:, J - 192 : J + 64].bitcast(BF16))
+            if q == 5:
+                staged.append(last[:, J - 320 : J - 64].bitcast(BF16))
+            elif q == 6:
+                staged.append(last[:, J - 64 : J + 192].bitcast(BF16))
             else:
                 staged.append(keep.tile([P, P * PACK], BF16, name="staged%d" % q, align_bytes=64)[:])
 
@@ -91,22 +97,24 @@ def tile_moe_expert_group_sums_wgrad_pl_kernel(tc, xf, xo, ra, rb, offs, offs2, 
         out_scales = out_2.rearrange("z q c -> (z q) c").bitcast(I32)
 
         def gather(q, out, first, columns):
-            nc.vector.tensor_copy(out, windows[q][:].indirect(lists[q][:, first : first + columns]))
+            width = max(2 * 16 * columns, 3 * T // 2)
+            window = tables[q][:, origin[q] : origin[q] + width]
+            nc.vector.tensor_copy(out, window.indirect(lists[q][:, first : first + columns]))
 
         def bank_tile(index, shape):
             return psum.tile(shape, F32, name="bank%d" % index, tag="bank%d" % index)
 
-        def sort_half(q, u):
+        def sort_first(q, first, columns):
             nc.scalar.copy(
-                sorted_of[q][:, :, 64 * u : 64 * (u + 1)].rearrange("k (t i) (h l) -> k t h i l", i=4, l=4),
-                gathered[q][:, half * u : half * (u + 1)].rearrange(
-                    "k (h l v t i) -> k v t h i l", l=4, v=2, t=2, i=4)[:, 0],
+                sorted_of[q][:, :, first : first + columns].rearrange("k i (h l) -> k h i l", l=4),
+                gathered[q][:, 16 * first : 16 * (first + columns)].rearrange(
+                    "k (h l t i) -> k t h i l", l=4, t=4, i=4)[:, 0],
             )
 
         def turn(q):
             bank = bank_tile(q % 4, [P, PACK, P])
             for t in range(PACK):
-                if q == 7 or t < 2:
+                if q == 7 or t == 0:
                     slots = sorted_of[q]
                 else:
                     slots = gathered[q][:].rearrange("k (p s) -> k s p", s=SLOTS)
@@ -151,9 +159,10 @@ def tile_moe_expert_group_sums_wgrad_pl_kernel(tc, xf, xo, ra, rb, offs, offs2, 
 
         banks = {}
         for q in range(PLANES - 1):
-            for u in range(2):
-                gather(q, gathered[q][:, half * u : half * (u + 1)], 64 * u, 64)
-                sort_half(q, u)
+            columns = 64 if q in (0, 6) else 128
+            for first in range(0, 128, columns):
+                gather(q, gathered[q][:, 16 * first : 16 * (first + columns)], first, columns)
+                sort_first(q, first, columns)
             if 1 <= q <= 5:
                 weigh_by_slots(q - 1, banks[q - 1])
             banks[q] = turn(q)
@@ -165,12 +174,12 @@ def tile_moe_expert_group_sums_wgrad_pl_kernel(tc, xf, xo, ra, rb, offs, offs2, 
                 pieces[u].rearrange("k (h l t i) -> k t h i l", l=4, t=4, i=4),
             )
         banks[7] = turn(7)
-        weigh_by_slots(5, banks[5])
         nc.vector.quantize_mx(out=b_codes[:].bitcast(E5M2), scales=b_scales[:], in_=staged_o[:])
         quantize(4)
+        weigh_whole(5, banks[5])
         weigh_whole(6, banks[6])
-        quantize(6)
         quantize(5)
+        quantize(6)
         weigh_whole(7, banks[7])
         quantize(7)
         for t, index in ((0, 1), (1, 4), (2, 5)):
@@ -182,13 +191,14 @@ def tile_moe_expert_group_sums_wgrad_pl_kernel(tc, xf, xo, ra, rb, offs, offs2, 
         for cols in halves:
             scale_out(3, acc3, cols)
         store_rows(3)
-        for cols in halves:
-            round_pair(2, cols)
+        round_pair(2, halves[0])
+        round_pair(2, slice(N // 2, 3 * N // 4))
+        nc.scalar.copy(y_round[:, 3 * N // 4 : N, 2:4], y[:, 2:4, 3 * N // 4 : N].rearrange("p t n -> p n t"))
         for cols in halves:
             nc.vector.quantize_mx(out=y_codes[:, cols].bitcast(E4M3), scales=y_scales[:, cols],
                                   in_=y_round[:, cols, :].rearrange("p n t -> p (n t)"))
             nc.sync.dma_start(out=out_words[:, cols], in_=y_codes[:, cols].bitcast(I32))
         for quad in range(4):
-            queue = nc.scalar if quad < 2 else nc.sync
+            queue = nc.scalar if quad < 3 else nc.sync
             queue.dma_start(out=out_scales[4 * quad : 4 * quad + 4, :],
                             in_=y_scales[32 * quad : 32 * quad + 4, :].bitcast(I32))

@@ -34,7 +34,7 @@ def tile_moe_expert_group_sums_wgrad_pl_kernel(tc, xf, xo, ra, rb, offs, offs2, 
 
         list_f = keep.tile([P, J // 16], U16, name="list_f")
         list_o = keep.tile([P, J // 16], U16, name="list_o")
-        table_o = keep.tile([P, 6 * T], F32, name="table_o")
+        table_o = keep.tile([P, 5 * T], F32, name="table_o")
         table_f = keep.tile([P, 5 * T], F32, name="table_f")
         tables = [table_o] * 4 + [table_f] * 4
         origin = [3 * T, 2 * T, T, 0, 0, T, 2 * T, 3 * T]
@@ -59,15 +59,15 @@ def tile_moe_expert_group_sums_wgrad_pl_kernel(tc, xf, xo, ra, rb, offs, offs2, 
         nc.sync.dma_start(out=weight_f[:], in_=ra.rearrange("o (p t) -> (o p) t", t=PACK))
         for q in range(4, PLANES):
             nc.sync.dma_start(out=windows[q], in_=sources[q])
-        nc.vector.memset(table_o[:, 4 * T : 6 * T], 0.0)
-        nc.vector.memset(table_f[:, 4 * T : 5 * T], 0.0)
+        nc.vector.memset(table_o[:, 4 * T : 5 * T].bitcast(I32), 0)
+        nc.vector.memset(table_f[:, 4 * T : 5 * T].bitcast(I32), 0)
         make_identity(nc, ident[:])
 
         gathered = [keep.tile([P, J], F32, name="gathered%d" % q) for q in range(PLANES - 1)]
         starts = [sum(LAST_PIECES[:u]) for u in range(len(LAST_PIECES))]
         last = keep.tile([P, J + 192], F32, name="last", align_bytes=64)
         pieces = [last[:, 16 * starts[u] : 16 * (starts[u] + LAST_PIECES[u])] for u in range(len(LAST_PIECES))]
-        quarter = J // 4
+        quarter = J // 2
         arena = keep.tile([P, quarter + J], F32, name="arena")
         sorted_of = [arena[:, quarter // 2 : quarter // 2 + quarter]] * 6
         sorted_of = sorted_of + [arena[:, 0:quarter], arena[:, quarter : quarter + J]]
@@ -106,15 +106,15 @@ def tile_moe_expert_group_sums_wgrad_pl_kernel(tc, xf, xo, ra, rb, offs, offs2, 
 
         def sort_first(q, first, columns):
             nc.scalar.copy(
-                sorted_of[q][:, :, first : first + columns].rearrange("k i (h l) -> k h i l", l=4),
+                sorted_of[q][:, :, first : first + columns].rearrange("k (t i) (h l) -> k t h i l", i=4, l=4),
                 gathered[q][:, 16 * first : 16 * (first + columns)].rearrange(
-                    "k (h l t i) -> k t h i l", l=4, t=4, i=4)[:, 0],
+                    "k (h l v t i) -> k v t h i l", l=4, v=2, t=2, i=4)[:, 0],
             )
 
         def turn(q):
-            bank = bank_tile(q % 4, [P, PACK, P])
-            for t in range(PACK):
-                if q == 7 or t == 0:
+            bank = bank_tile((0, 1, 2, 3, 0, 1, 0, 3)[q], [P, PACK, P])
+            for t in (2, 3, 0, 1) if q == 6 else range(PACK):
+                if q == 7 or t < 2:
                     slots = sorted_of[q]
                 else:
                     slots = gathered[q][:].rearrange("k (p s) -> k s p", s=SLOTS)
@@ -159,7 +159,7 @@ def tile_moe_expert_group_sums_wgrad_pl_kernel(tc, xf, xo, ra, rb, offs, offs2, 
 
         banks = {}
         for q in range(PLANES - 1):
-            columns = 64 if q in (0, 6) else 128
+            columns = 64 if q in (0, 1, 6) else 128
             for first in range(0, 128, columns):
                 gather(q, gathered[q][:, 16 * first : 16 * (first + columns)], first, columns)
                 sort_first(q, first, columns)

@@ -16,6 +16,7 @@ E4M3 = mybir.dt.float8_e4m3fn_x4
 E5M2 = mybir.dt.float8_e5m2_x4
 COPY = mybir.ActivationFunctionType.Copy
 MULT = mybir.AluOpType.mult
+ADD = mybir.AluOpType.add
 
 P = 128
 PACK = 4
@@ -23,7 +24,6 @@ GROUP = J // B
 SLOTS = PACK * GROUP
 PLANES = 8
 OUT_SCALE = 0.03
-LAST_PIECES = (56, 36, 24, 12)
 
 
 def tile_moe_expert_group_sums_wgrad_pl_kernel(tc, xf, xo, ra, rb, offs, offs2, out_0, out_1, out_2):
@@ -63,25 +63,15 @@ def tile_moe_expert_group_sums_wgrad_pl_kernel(tc, xf, xo, ra, rb, offs, offs2, 
         nc.vector.memset(table_f[:, 4 * T : 5 * T].bitcast(I32), 0)
         make_identity(nc, ident[:])
 
-        gathered = [keep.tile([P, J], F32, name="gathered%d" % q) for q in range(PLANES - 1)]
-        starts = [sum(LAST_PIECES[:u]) for u in range(len(LAST_PIECES))]
-        last = keep.tile([P, J + 192], F32, name="last", align_bytes=64)
-        pieces = [last[:, 16 * starts[u] : 16 * (starts[u] + LAST_PIECES[u])] for u in range(len(LAST_PIECES))]
-        quarter = J // 2
-        arena = keep.tile([P, quarter + J], F32, name="arena")
-        sorted_of = [arena[:, quarter // 2 : quarter // 2 + quarter]] * 6
-        sorted_of = sorted_of + [arena[:, 0:quarter], arena[:, quarter : quarter + J]]
-        sorted_of = [s.rearrange("k (s p) -> k s p", p=P) for s in sorted_of]
+        gathered = [keep.tile([P, J], F32, name="gathered%d" % q) for q in range(PLANES)]
+        sorted_slots = keep.tile([P, SLOTS // 2, P], F32, name="sorted_slots")
+        pairs = keep.tile([P, J // 4], F32, name="pairs")
+        sums = keep.tile([P, PACK, P], F32, name="sums")
 
         staged_o = keep.tile([P, N * PACK], BF16, name="staged_o", align_bytes=64)
         staged = [staged_o[:, q * P * PACK : (q + 1) * P * PACK] for q in range(4)]
         for q in range(4, PLANES):
-            if q == 5:
-                staged.append(last[:, J - 320 : J - 64].bitcast(BF16))
-            elif q == 6:
-                staged.append(last[:, J - 64 : J + 192].bitcast(BF16))
-            else:
-                staged.append(keep.tile([P, P * PACK], BF16, name="staged%d" % q, align_bytes=64)[:])
+            staged.append(keep.tile([P, P * PACK], BF16, name="staged%d" % q, align_bytes=64)[:])
 
         b_codes = keep.tile([P, N], U32, name="b_codes", align_bytes=64)
         b_scales = keep.tile([P, N], U8, name="b_scales", align_bytes=64)
@@ -106,26 +96,24 @@ def tile_moe_expert_group_sums_wgrad_pl_kernel(tc, xf, xo, ra, rb, offs, offs2, 
 
         def sort_first(q, first, columns):
             nc.scalar.copy(
-                sorted_of[q][:, :, first : first + columns].rearrange("k (t i) (h l) -> k t h i l", i=4, l=4),
+                sorted_slots[:, :, first : first + columns].rearrange("k (t i) (h l) -> k t h i l", i=4, l=4),
                 gathered[q][:, 16 * first : 16 * (first + columns)].rearrange(
                     "k (h l v t i) -> k v t h i l", l=4, v=2, t=2, i=4)[:, 0],
             )
 
-        def turn(q):
-            bank = bank_tile((0, 1, 2, 3, 0, 1, 0, 3)[q], [P, PACK, P])
-            for t in (2, 3, 0, 1) if q == 6 else range(PACK):
-                if q == 7 or t < 2:
-                    slots = sorted_of[q]
+        def turn(q, bank, order):
+            for t in order:
+                if t < 2:
+                    slots = sorted_slots
                 else:
                     slots = gathered[q][:].rearrange("k (p s) -> k s p", s=SLOTS)
                 for i in range(GROUP):
                     nc.tensor.matmul(bank[:, t, :], lhsT=slots[:, GROUP * t + i, :], rhs=ident[:], is_transpose=True,
                                      start=(i == 0), stop=(i == GROUP - 1))
-            return bank
 
-        def weigh_by_slots(q, bank):
+        def weigh_by_slots(q, bank, order):
             words = staged[q].rearrange("p (k t) -> p t k", t=PACK)
-            for t in range(PACK):
+            for t in order:
                 nc.scalar.activation(words[:, t, :], bank[:, t, :], COPY, scale=weights[q][:, t : t + 1])
 
         def weigh_whole(q, bank):
@@ -163,26 +151,36 @@ def tile_moe_expert_group_sums_wgrad_pl_kernel(tc, xf, xo, ra, rb, offs, offs2, 
             for first in range(0, 128, columns):
                 gather(q, gathered[q][:, 16 * first : 16 * (first + columns)], first, columns)
                 sort_first(q, first, columns)
-            if 1 <= q <= 5:
-                weigh_by_slots(q - 1, banks[q - 1])
-            banks[q] = turn(q)
-        for u in range(len(LAST_PIECES)):
-            gather(7, pieces[u], starts[u], LAST_PIECES[u])
-            nc.scalar.copy(
-                sorted_of[7][:, :, starts[u] : starts[u] + LAST_PIECES[u]].rearrange(
-                    "k (t i) (h l) -> k t h i l", i=4, l=4),
-                pieces[u].rearrange("k (h l t i) -> k t h i l", l=4, t=4, i=4),
-            )
-        banks[7] = turn(7)
+            if q >= 1:
+                weigh_by_slots(q - 1, banks[q - 1], range(PACK))
+            if q < 6:
+                banks[q] = bank_tile(q % 4, [P, PACK, P])
+                turn(q, banks[q], range(PACK))
+        for index, order in ((0, (2, 3)), (2, (0, 1))):
+            bank = bank_tile(index, [P, PACK, P])
+            turn(6, bank, order)
+            weigh_by_slots(6, bank, order)
+        for first in (0, 64):
+            gather(7, gathered[7][:, 16 * first : 16 * (first + 64)], first, 64)
+        early = gathered[7][:, 0 : J // 2].rearrange("k (b v e) -> k v b e", v=2, e=2)
+        nc.gpsimd.tensor_tensor(pairs[:].rearrange("k (b e) -> k b e", e=2), early[:, 0], early[:, 1], ADD)
+        paired = pairs[:].rearrange("k (h l t e) -> k e h t l", l=4, t=4, e=2)
+        nc.gpsimd.tensor_tensor(sums[:, :, 0:64].rearrange("k t (h l) -> k h t l", l=4), paired[:, 0], paired[:, 1], ADD)
+        nc.vector.tensor_reduce(
+            sums[:, :, 64:128].rearrange("k t (h l) -> k h t l", l=4),
+            gathered[7][:, J // 2 : J].rearrange("k (h l t i) -> k h t l i", l=4, t=4, i=4),
+            axis=mybir.AxisListType.X, op=ADD,
+        )
+        bank7 = bank_tile(1, [P, PACK, P])
+        for t in range(PACK):
+            nc.tensor.transpose(bank7[:, t, :], sums[:, t, :], ident[:])
         nc.vector.quantize_mx(out=b_codes[:].bitcast(E5M2), scales=b_scales[:], in_=staged_o[:])
         quantize(4)
-        weigh_whole(5, banks[5])
-        weigh_whole(6, banks[6])
         quantize(5)
+        weigh_whole(7, bank7)
         quantize(6)
-        weigh_whole(7, banks[7])
         quantize(7)
-        for t, index in ((0, 1), (1, 4), (2, 5)):
+        for t, index in ((0, 0), (1, 2), (2, 5)):
             scale_out(t, product(t, index), whole)
             store_rows(t)
             if t == 1:

from contextlib import ExitStack

import concourse.mybir as mybir
from concourse.masks import make_identity

K, N, T, J, B = 512, 512, 1024, 2048, 512
FLOPS = 2 * K * N * B

F32 = mybir.dt.float32
BF16 = mybir.dt.bfloat16
I32 = mybir.dt.int32
U32 = mybir.dt.uint32
U16 = mybir.dt.uint16
U8 = mybir.dt.uint8
E4M3 = mybir.dt.float8_e4m3fn_x4
E5M2 = mybir.dt.float8_e5m2_x4
COPY = mybir.ActivationFunctionType.Copy
MULT = mybir.AluOpType.mult
ADD = mybir.AluOpType.add

P = 128
PACK = 4
GROUP = J // B
SLOTS = PACK * GROUP
PLANES = 8
OUT_SCALE = 0.03


def tile_moe_expert_group_sums_wgrad_pl_kernel(tc, xf, xo, ra, rb, offs, offs2, out_0, out_1, out_2):
    nc = tc.nc
    with ExitStack() as ctx:
        keep = ctx.enter_context(tc.tile_pool(name="keep", bufs=1))
        psum = ctx.enter_context(tc.psum_pool(name="psum", bufs=1))

        list_f = keep.tile([P, J // 16], U16, name="list_f")
        list_o = keep.tile([P, J // 16], U16, name="list_o")
        table_o = keep.tile([P, 5 * T], F32, name="table_o")
        table_f = keep.tile([P, 5 * T], F32, name="table_f")
        tables = [table_o] * 4 + [table_f] * 4
        origin = [3 * T, 2 * T, T, 0, 0, T, 2 * T, 3 * T]
        windows = [tables[q][:, origin[q] : origin[q] + T] for q in range(PLANES)]
        weight_f = keep.tile([P, PACK], F32, name="weight_f")
        weight_o = keep.tile([P, PACK], F32, name="weight_o")
        ident = keep.tile([P, P], F32, name="ident")

        xo_planes = xo.rearrange("(c p) s -> c p s", p=P)
        xf_planes = xf.rearrange("(p t) s -> t p s", t=PACK)
        sources = [xo_planes[c] for c in range(4)] + [xf_planes[t] for t in range(4)]
        lists = [list_o] * 4 + [list_f] * 4
        weights = [weight_o] * 4 + [weight_f] * 4

        nc.sync.dma_start(list_o[:], offs2)
        nc.sync.dma_start(out=windows[0], in_=sources[0])
        nc.sync.dma_start(out=windows[1], in_=sources[1])
        nc.sync.dma_start(out=weight_o[:], in_=rb.rearrange("o (p t) -> (o p) t", t=PACK))
        nc.sync.dma_start(out=windows[2], in_=sources[2])
        nc.sync.dma_start(out=windows[3], in_=sources[3])
        nc.sync.dma_start(list_f[:], offs)
        nc.sync.dma_start(out=weight_f[:], in_=ra.rearrange("o (p t) -> (o p) t", t=PACK))
        for q in range(4, PLANES):
            nc.sync.dma_start(out=windows[q], in_=sources[q])
        nc.vector.memset(table_o[:, 4 * T : 5 * T].bitcast(I32), 0)
        nc.vector.memset(table_f[:, 4 * T : 5 * T].bitcast(I32), 0)
        make_identity(nc, ident[:])

        gathered = [keep.tile([P, J], F32, name="gathered%d" % q) for q in range(PLANES)]
        sorted_slots = keep.tile([P, SLOTS // 2, P], F32, name="sorted_slots")
        pairs = keep.tile([P, J // 4], F32, name="pairs")
        sums = keep.tile([P, PACK, P], F32, name="sums")

        staged_o = keep.tile([P, N * PACK], BF16, name="staged_o", align_bytes=64)
        staged = [staged_o[:, q * P * PACK : (q + 1) * P * PACK] for q in range(4)]
        for q in range(4, PLANES):
            staged.append(keep.tile([P, P * PACK], BF16, name="staged%d" % q, align_bytes=64)[:])

        b_codes = keep.tile([P, N], U32, name="b_codes", align_bytes=64)
        b_scales = keep.tile([P, N], U8, name="b_scales", align_bytes=64)
        a_codes = [keep.tile([P, P], U32, name="a_codes%d" % t, align_bytes=64) for t in range(PACK)]
        a_scales = [keep.tile([P, P], U8, name="a_scales%d" % t, align_bytes=64) for t in range(PACK)]

        y = keep.tile([P, PACK, N], F32, name="y")
        y_round = keep.tile([P, N, PACK], BF16, name="y_round", align_bytes=64)
        y_codes = keep.tile([P, N], U32, name="y_codes", align_bytes=64)
        y_scales = keep.tile([P, N], U8, name="y_scales", align_bytes=64)
        out_rows = out_0.rearrange("(m t) n -> t m n", t=PACK)
        out_words = out_1.rearrange("z l c r -> (z l) (c r)").bitcast(I32)
        out_scales = out_2.rearrange("z q c -> (z q) c").bitcast(I32)

        def gather(q, out, first, columns):
            width = max(2 * 16 * columns, 3 * T // 2)
            window = tables[q][:, origin[q] : origin[q] + width]
            nc.vector.tensor_copy(out, window.indirect(lists[q][:, first : first + columns]))

        def bank_tile(index, shape):
            return psum.tile(shape, F32, name="bank%d" % index, tag="bank%d" % index)

        def sort_first(q, first, columns):
            nc.scalar.copy(
                sorted_slots[:, :, first : first + columns].rearrange("k (t i) (h l) -> k t h i l", i=4, l=4),
                gathered[q][:, 16 * first : 16 * (first + columns)].rearrange(
                    "k (h l v t i) -> k v t h i l", l=4, v=2, t=2, i=4)[:, 0],
            )

        def turn(q, bank, order):
            for t in order:
                if t < 2:
                    slots = sorted_slots
                else:
                    slots = gathered[q][:].rearrange("k (p s) -> k s p", s=SLOTS)
                for i in range(GROUP):
                    nc.tensor.matmul(bank[:, t, :], lhsT=slots[:, GROUP * t + i, :], rhs=ident[:], is_transpose=True,
                                     start=(i == 0), stop=(i == GROUP - 1))

        def weigh_by_slots(q, bank, order):
            words = staged[q].rearrange("p (k t) -> p t k", t=PACK)
            for t in order:
                nc.scalar.activation(words[:, t, :], bank[:, t, :], COPY, scale=weights[q][:, t : t + 1])

        def weigh_whole(q, bank):
            nc.vector.tensor_tensor(
                staged[q].rearrange("p (k t) -> p k t", t=PACK),
                bank[:].rearrange("p t k -> p k t"),
                weights[q][:].unsqueeze(1).to_broadcast([P, P, PACK]),
                MULT,
            )

        def quantize(q):
            nc.vector.quantize_mx(out=a_codes[q - 4][:].bitcast(E4M3), scales=a_scales[q - 4][:], in_=staged[q])

        def product(t, index):
            acc = bank_tile(index, [P, N])
            nc.tensor.matmul_mx(out=acc[:], lhsT=a_codes[t][:].bitcast(E4M3), lhsT_scale=a_scales[t][:],
                                rhs=b_codes[:].bitcast(E5M2), rhs_scale=b_scales[:], start=True, stop=True)
            return acc

        def scale_out(t, acc, cols):
            nc.scalar.activation(y[:, t, cols], acc[:, cols], COPY, scale=OUT_SCALE)

        def store_rows(t):
            nc.sync.dma_start(out=out_rows[t], in_=y[:, t, :])

        def round_pair(t, cols):
            nc.vector.tensor_copy(y_round[:, cols, t : t + 2], y[:, t : t + 2, cols].rearrange("p t n -> p n t"))

        whole = slice(0, N)
        halves = (slice(0, N // 2), slice(N // 2, N))

        banks = {}
        for q in range(PLANES - 1):
            columns = 64 if q in (0, 1, 6) else 128
            for first in range(0, 128, columns):
                gather(q, gathered[q][:, 16 * first : 16 * (first + columns)], first, columns)
                sort_first(q, first, columns)
            if q >= 1:
                weigh_by_slots(q - 1, banks[q - 1], range(PACK))
            if q < 6:
                banks[q] = bank_tile(q % 4, [P, PACK, P])
                turn(q, banks[q], range(PACK))
        for index, order in ((0, (2, 3)), (2, (0, 1))):
            bank = bank_tile(index, [P, PACK, P])
            turn(6, bank, order)
            weigh_by_slots(6, bank, order)
        for first in (0, 64):
            gather(7, gathered[7][:, 16 * first : 16 * (first + 64)], first, 64)
        early = gathered[7][:, 0 : J // 2].rearrange("k (b v e) -> k v b e", v=2, e=2)
        nc.gpsimd.tensor_tensor(pairs[:].rearrange("k (b e) -> k b e", e=2), early[:, 0], early[:, 1], ADD)
        paired = pairs[:].rearrange("k (h l t e) -> k e h t l", l=4, t=4, e=2)
        nc.gpsimd.tensor_tensor(sums[:, :, 0:64].rearrange("k t (h l) -> k h t l", l=4), paired[:, 0], paired[:, 1], ADD)
        nc.vector.tensor_reduce(
            sums[:, :, 64:128].rearrange("k t (h l) -> k h t l", l=4),
            gathered[7][:, J // 2 : J].rearrange("k (h l t i) -> k h t l i", l=4, t=4, i=4),
            axis=mybir.AxisListType.X, op=ADD,
        )
        bank7 = bank_tile(1, [P, PACK, P])
        for t in range(PACK):
            nc.tensor.transpose(bank7[:, t, :], sums[:, t, :], ident[:])
        nc.vector.quantize_mx(out=b_codes[:].bitcast(E5M2), scales=b_scales[:], in_=staged_o[:])
        quantize(4)
        quantize(5)
        weigh_whole(7, bank7)
        quantize(6)
        quantize(7)
        for t, index in ((0, 0), (1, 2), (2, 5)):
            scale_out(t, product(t, index), whole)
            store_rows(t)
            if t == 1:
                round_pair(0, whole)
        acc3 = product(3, 6)
        for cols in halves:
            scale_out(3, acc3, cols)
        store_rows(3)
        round_pair(2, halves[0])
        round_pair(2, slice(N // 2, 3 * N // 4))
        nc.scalar.copy(y_round[:, 3 * N // 4 : N, 2:4], y[:, 2:4, 3 * N // 4 : N].rearrange("p t n -> p n t"))
        for cols in halves:
            nc.vector.quantize_mx(out=y_codes[:, cols].bitcast(E4M3), scales=y_scales[:, cols],
                                  in_=y_round[:, cols, :].rearrange("p n t -> p (n t)"))
            nc.sync.dma_start(out=out_words[:, cols], in_=y_codes[:, cols].bitcast(I32))
        for quad in range(4):
            queue = nc.scalar if quad < 3 else nc.sync
            queue.dma_start(out=out_scales[4 * quad : 4 * quad + 4, :],
                            in_=y_scales[32 * quad : 32 * quad + 4, :].bitcast(I32))
